import numpy as np
import ml_dtypes

BF16 = ml_dtypes.bfloat16


def bf(x):
    return np.asarray(x, np.float32).astype(BF16)


def f32(x):
    return np.asarray(x, np.float32)


def f64(x):
    return np.asarray(x).astype(np.float64)


def striped(idx):
    return np.tile(idx.reshape(-1, 16).T, (8, 1))


def rows(idx, k):
    return np.tile(idx, (k, 1))


def look(tab, idx):
    return np.take_along_axis(f64(tab), rows(idx, len(tab)), axis=1)


K, S, D, V, N = 256, 2048, 2, 1024, 2048


def setup_inputs():
    return {"tab": f32(np.random.standard_normal((K, S))), "x0": f32(1.0 * np.random.standard_normal((K, V))), "offs": striped(np.random.permutation(S)[:N])}


def reference(tab, x0, offs):
    idx = offs[:16].T.reshape(-1)
    a = (f64(x0) + sum(look(tab, idx[d * V:(d + 1) * V]) for d in range(D))) / (D + 1)
    x = ((f64(x0) - a) ** 2 + sum((look(tab, idx[d * V:(d + 1) * V]) - a) ** 2 for d in range(D))) / (D + 1)
    return x

@@ -1,0 +1,69 @@
+from contextlib import ExitStack
+
+import concourse.mybir as mybir
+from concourse.masks import make_identity
+
+F32, U16 = mybir.dt.float32, mybir.dt.uint16
+ADD, SUBTRACT = mybir.AluOpType.add, mybir.AluOpType.subtract
+COPY, SQUARE = mybir.ActivationFunctionType.Copy, mybir.ActivationFunctionType.Square
+
+P = 128
+PIECE = 512
+GROUP = 16
+
+
+def tile_lookup_vari_out_kernel(tc, tab, x0, offs, out):
+    nc = tc.nc
+    rows, slots = tab.shape
+    nodes = x0.shape[1]
+    neighbours = offs.shape[1] * GROUP // nodes
+    blocks, pieces = rows // P, nodes // PIECE
+    third = 1.0 / (neighbours + 1)
+
+    with ExitStack() as ctx:
+        held = ctx.enter_context(tc.tile_pool(name="held", bufs=1))
+        work = ctx.enter_context(tc.tile_pool(name="work", bufs=blocks * pieces))
+        psum = ctx.enter_context(tc.psum_pool(name="psum", bufs=blocks * pieces))
+
+        offsets = held.tile(list(offs.shape), U16, name="offsets")
+        nc.sync.dma_start(offsets[:], offs)
+        identity = held.tile([P, P], F32, name="identity")
+        make_identity(nc, identity[:])
+
+        windows, own = [], {}
+        for b in range(blocks):
+            window = held.tile([P, slots], F32, name=f"window{b}")
+            nc.sync.dma_start(window[:], tab[b * P : (b + 1) * P, :])
+            windows.append(window)
+            for k in range(pieces):
+                own[b, k] = held.tile([P, PIECE], F32, name=f"own{b}_{k}")
+                nc.sync.dma_start(own[b, k][:], x0[b * P : (b + 1) * P, k * PIECE : (k + 1) * PIECE])
+
+        def neighbour(b, d, k):
+            first = (d * nodes + k * PIECE) // GROUP
+            return windows[b][:].indirect(offsets[:, first : first + PIECE // GROUP])
+
+        for b in range(blocks):
+            sums = {k: own[b, k] for k in range(pieces)}
+            for d in range(neighbours):
+                for k in range(pieces):
+                    total = work.tile([P, PIECE], F32, name=f"total{d}")
+                    nc.vector.tensor_tensor(total[:], neighbour(b, d, k), sums[k][:], ADD)
+                    sums[k] = total
+
+            for k in range(pieces):
+                mean = work.tile([P, PIECE], F32, name="mean")
+                nc.scalar.activation(mean[:], sums[k][:], COPY, scale=third)
+
+                squares = psum.tile([P, PIECE], F32, name="squares")
+                for d in range(neighbours + 1):
+                    value = own[b, k][:] if d == 0 else neighbour(b, d - 1, k)
+                    diff = work.tile([P, PIECE], F32, name=f"diff{d}")
+                    nc.vector.tensor_tensor(diff[:], value, mean[:], SUBTRACT)
+                    square = work.tile([P, PIECE], F32, name=f"square{d}")
+                    nc.scalar.activation(square[:], diff[:], SQUARE)
+                    nc.tensor.matmul(squares[:], identity[:], square[:], start=d == 0, stop=d == neighbours)
+
+                result = work.tile([P, PIECE], F32, name="result")
+                nc.scalar.activation(result[:], squares[:], COPY, scale=third)
+                nc.sync.dma_start(out[b * P : (b + 1) * P, k * PIECE : (k + 1) * PIECE], result[:])

@@ -1,3 +1,4 @@
+import math
 from contextlib import ExitStack
 
 import concourse.mybir as mybir
@@ -8,62 +9,101 @@ ADD, SUBTRACT = mybir.AluOpType.add, mybir.AluOpType.subtract
 COPY, SQUARE = mybir.ActivationFunctionType.Copy, mybir.ActivationFunctionType.Square
 
 P = 128
-PIECE = 512
+BANK = 512
 GROUP = 16
+THIRD = 1.0 / 3.0
 
 
 def tile_lookup_vari_out_kernel(tc, tab, x0, offs, out):
     nc = tc.nc
-    rows, slots = tab.shape
-    nodes = x0.shape[1]
-    neighbours = offs.shape[1] * GROUP // nodes
-    blocks, pieces = rows // P, nodes // PIECE
-    third = 1.0 / (neighbours + 1)
+    slots, nodes = tab.shape[1], x0.shape[1]
+    half = BANK // 2
+
+    pieces = [(0, 0, BANK), (0, BANK, BANK), (1, 0, BANK), (1, BANK, half), (1, BANK + half, half)]
+    count = len(pieces)
+    in_block = [[i for i in range(count) if pieces[i][0] == block] for block in range(2)]
+    on_vector = range(count - 3, count)
 
     with ExitStack() as ctx:
         held = ctx.enter_context(tc.tile_pool(name="held", bufs=1))
-        work = ctx.enter_context(tc.tile_pool(name="work", bufs=blocks * pieces))
-        psum = ctx.enter_context(tc.psum_pool(name="psum", bufs=blocks * pieces))
+        diff_ring = ctx.enter_context(tc.tile_pool(name="diff_ring", bufs=3))
+        square_ring = ctx.enter_context(tc.tile_pool(name="square_ring", bufs=3))
+        psum = ctx.enter_context(tc.psum_pool(name="psum", bufs=1))
+
+        def piece_tile(name, i, pool=held):
+            return pool.tile([P, pieces[i][2]], F32, name=f"{name}_{i}")
+
+        def in_dram(array, i):
+            block, first, width = pieces[i]
+            return array[block * P : (block + 1) * P, first : first + width]
 
         offsets = held.tile(list(offs.shape), U16, name="offsets")
         nc.sync.dma_start(offsets[:], offs)
         identity = held.tile([P, P], F32, name="identity")
         make_identity(nc, identity[:])
+        minus_third = held.tile([P, P], F32, name="minus_third")
+        nc.gpsimd.tensor_scalar_mul(minus_third[:], identity[:], -THIRD)
 
-        windows, own = [], {}
-        for b in range(blocks):
-            window = held.tile([P, slots], F32, name=f"window{b}")
-            nc.sync.dma_start(window[:], tab[b * P : (b + 1) * P, :])
-            windows.append(window)
-            for k in range(pieces):
-                own[b, k] = held.tile([P, PIECE], F32, name=f"own{b}_{k}")
-                nc.sync.dma_start(own[b, k][:], x0[b * P : (b + 1) * P, k * PIECE : (k + 1) * PIECE])
+        windows, own = {}, {}
+        for block in range(2):
+            windows[block] = held.tile([P, slots], F32, name=f"window{block}")
+            nc.sync.dma_start(windows[block][:], tab[block * P : (block + 1) * P, :])
+            for i in in_block[block]:
+                own[i] = piece_tile("own", i)
+                nc.sync.dma_start(own[i][:], in_dram(x0, i))
 
-        def neighbour(b, d, k):
-            first = (d * nodes + k * PIECE) // GROUP
-            return windows[b][:].indirect(offsets[:, first : first + PIECE // GROUP])
+        def neighbour(i, d):
+            block, first, width = pieces[i]
+            column = (d * nodes + first) // GROUP
+            return windows[block][:].indirect(offsets[:, column : column + width // GROUP])
 
-        for b in range(blocks):
-            sums = {k: own[b, k] for k in range(pieces)}
-            for d in range(neighbours):
-                for k in range(pieces):
-                    total = work.tile([P, PIECE], F32, name=f"total{d}")
-                    nc.vector.tensor_tensor(total[:], neighbour(b, d, k), sums[k][:], ADD)
-                    sums[k] = total
+        pair, mean, own_diff, variance, squares = {}, {}, {}, {}, {}
 
-            for k in range(pieces):
-                mean = work.tile([P, PIECE], F32, name="mean")
-                nc.scalar.activation(mean[:], sums[k][:], COPY, scale=third)
+        for block in range(2):
+            for i in in_block[block]:
+                own_diff[i] = piece_tile("own_diff", i, psum)
+                nc.tensor.matmul(own_diff[i][:], identity[:], own[i][:], start=True, stop=False)
+            for i in in_block[block]:
+                pair[i] = piece_tile("pair", i)
+                nc.vector.tensor_tensor(pair[i][:], neighbour(i, 0), own[i][:], ADD)
+            for i in in_block[block]:
+                total = piece_tile("total", i)
+                nc.vector.tensor_tensor(total[:], neighbour(i, 1), pair[i][:], ADD)
+                mean[i] = piece_tile("mean", i)
+                nc.scalar.activation(mean[i][:], total[:], COPY, scale=THIRD)
+                nc.tensor.matmul(own_diff[i][:], minus_third[:], total[:], start=False, stop=True)
 
-                squares = psum.tile([P, PIECE], F32, name="squares")
-                for d in range(neighbours + 1):
-                    value = own[b, k][:] if d == 0 else neighbour(b, d - 1, k)
-                    diff = work.tile([P, PIECE], F32, name=f"diff{d}")
-                    nc.vector.tensor_tensor(diff[:], value, mean[:], SUBTRACT)
-                    square = work.tile([P, PIECE], F32, name=f"square{d}")
-                    nc.scalar.activation(square[:], diff[:], SQUARE)
-                    nc.tensor.matmul(squares[:], identity[:], square[:], start=d == 0, stop=d == neighbours)
+        def add_square(i, term, diff):
+            if i in on_vector:
+                square = squares[i, term] = piece_tile(f"square{term}", i)
+            else:
+                square = square_ring.tile([P, pieces[i][2]], F32, name="square")
+            nc.scalar.activation(square[:], diff[:], SQUARE, scale=math.sqrt(THIRD))
+            if i not in on_vector:
+                if term == 0:
+                    variance[i] = piece_tile("variance", i, psum)
+                nc.tensor.matmul(variance[i][:], identity[:], square[:], start=term == 0, stop=term == 2)
 
-                result = work.tile([P, PIECE], F32, name="result")
-                nc.scalar.activation(result[:], squares[:], COPY, scale=third)
-                nc.sync.dma_start(out[b * P : (b + 1) * P, k * PIECE : (k + 1) * PIECE], result[:])
+        def neighbour_diff(i, d):
+            diff = diff_ring.tile([P, pieces[i][2]], F32, name="diff")
+            nc.vector.tensor_tensor(diff[:], neighbour(i, d), mean[i][:], SUBTRACT)
+            return diff
+
+        def finish(i):
+            result = piece_tile("result", i)
+            if i in on_vector:
+                partial = piece_tile("partial", i)
+                nc.vector.tensor_tensor(partial[:], squares[i, 0][:], squares[i, 1][:], ADD)
+                nc.vector.tensor_tensor(result[:], partial[:], squares[i, 2][:], ADD)
+            else:
+                nc.scalar.activation(result[:], variance[i][:], COPY)
+            nc.sync.dma_start(in_dram(out, i), result[:])
+
+        for i in range(count):
+            add_square(i, 0, own_diff[i])
+        for i in range(count):
+            add_square(i, 1, neighbour_diff(i, 0))
+            if i > 0:
+                finish(i - 1)
+            add_square(i, 2, neighbour_diff(i, 1))
+        finish(count - 1)

@@ -19,7 +19,7 @@ def tile_lookup_vari_out_kernel(tc, tab, x0, offs, out):
     slots, nodes = tab.shape[1], x0.shape[1]
     half = BANK // 2
 
-    pieces = [(0, 0, BANK), (0, BANK, BANK), (1, 0, BANK), (1, BANK, half), (1, BANK + half, half)]
+    pieces = [(0, 0, half), (0, half, half), (0, BANK, BANK), (1, 0, BANK), (1, BANK, half), (1, BANK + half, half)]
     count = len(pieces)
     in_block = [[i for i in range(count) if pieces[i][0] == block] for block in range(2)]
     on_vector = range(count - 3, count)
@@ -27,11 +27,13 @@ def tile_lookup_vari_out_kernel(tc, tab, x0, offs, out):
     with ExitStack() as ctx:
         held = ctx.enter_context(tc.tile_pool(name="held", bufs=1))
         diff_ring = ctx.enter_context(tc.tile_pool(name="diff_ring", bufs=3))
-        square_ring = ctx.enter_context(tc.tile_pool(name="square_ring", bufs=3))
-        psum = ctx.enter_context(tc.psum_pool(name="psum", bufs=1))
+        psum = ctx.enter_context(tc.psum_pool(name="psum", bufs=8))
 
-        def piece_tile(name, i, pool=held):
-            return pool.tile([P, pieces[i][2]], F32, name=f"{name}_{i}")
+        def piece_tile(name, i):
+            return held.tile([P, pieces[i][2]], F32, name=f"{name}_{i}")
+
+        def psum_tile(i):
+            return psum.tile([P, pieces[i][2]], F32, name="bank")
 
         def in_dram(array, i):
             block, first, width = pieces[i]
@@ -41,8 +43,8 @@ def tile_lookup_vari_out_kernel(tc, tab, x0, offs, out):
         nc.sync.dma_start(offsets[:], offs)
         identity = held.tile([P, P], F32, name="identity")
         make_identity(nc, identity[:])
-        minus_third = held.tile([P, P], F32, name="minus_third")
-        nc.gpsimd.tensor_scalar_mul(minus_third[:], identity[:], -THIRD)
+        minus_identity = held.tile([P, P], F32, name="minus_identity")
+        nc.gpsimd.tensor_scalar_mul(minus_identity[:], identity[:], -1.0)
 
         windows, own = {}, {}
         for block in range(2):
@@ -61,7 +63,7 @@ def tile_lookup_vari_out_kernel(tc, tab, x0, offs, out):
 
         for block in range(2):
             for i in in_block[block]:
-                own_diff[i] = piece_tile("own_diff", i, psum)
+                own_diff[i] = psum_tile(i)
                 nc.tensor.matmul(own_diff[i][:], identity[:], own[i][:], start=True, stop=False)
             for i in in_block[block]:
                 pair[i] = piece_tile("pair", i)
@@ -71,17 +73,14 @@ def tile_lookup_vari_out_kernel(tc, tab, x0, offs, out):
                 nc.vector.tensor_tensor(total[:], neighbour(i, 1), pair[i][:], ADD)
                 mean[i] = piece_tile("mean", i)
                 nc.scalar.activation(mean[i][:], total[:], COPY, scale=THIRD)
-                nc.tensor.matmul(own_diff[i][:], minus_third[:], total[:], start=False, stop=True)
+                nc.tensor.matmul(own_diff[i][:], minus_identity[:], mean[i][:], start=False, stop=True)
 
         def add_square(i, term, diff):
-            if i in on_vector:
-                square = squares[i, term] = piece_tile(f"square{term}", i)
-            else:
-                square = square_ring.tile([P, pieces[i][2]], F32, name="square")
+            square = squares[i, term] = piece_tile(f"square{term}", i)
             nc.scalar.activation(square[:], diff[:], SQUARE, scale=math.sqrt(THIRD))
             if i not in on_vector:
                 if term == 0:
-                    variance[i] = piece_tile("variance", i, psum)
+                    variance[i] = psum_tile(i)
                 nc.tensor.matmul(variance[i][:], identity[:], square[:], start=term == 0, stop=term == 2)
 
         def neighbour_diff(i, d):
@@ -101,7 +100,6 @@ def tile_lookup_vari_out_kernel(tc, tab, x0, offs, out):
 
         for i in range(count):
             add_square(i, 0, own_diff[i])
-        for i in range(count):
             add_square(i, 1, neighbour_diff(i, 0))
             if i > 0:
                 finish(i - 1)

@@ -94,9 +94,10 @@ def tile_lookup_vari_out_kernel(tc, tab, x0, offs, out):
                 partial = piece_tile("partial", i)
                 nc.vector.tensor_tensor(partial[:], squares[i, 0][:], squares[i, 1][:], ADD)
                 nc.vector.tensor_tensor(result[:], partial[:], squares[i, 2][:], ADD)
+                nc.sync.dma_start(in_dram(out, i), result[:])
             else:
                 nc.scalar.activation(result[:], variance[i][:], COPY)
-            nc.sync.dma_start(in_dram(out, i), result[:])
+                nc.scalar.dma_start(in_dram(out, i), result[:])
 
         for i in range(count):
             add_square(i, 0, own_diff[i])

import math
from contextlib import ExitStack

import concourse.mybir as mybir
from concourse.masks import make_identity

F32, U16 = mybir.dt.float32, mybir.dt.uint16
ADD, SUBTRACT = mybir.AluOpType.add, mybir.AluOpType.subtract
COPY, SQUARE = mybir.ActivationFunctionType.Copy, mybir.ActivationFunctionType.Square

P = 128
BANK = 512
GROUP = 16
THIRD = 1.0 / 3.0


def tile_lookup_vari_out_kernel(tc, tab, x0, offs, out):
    nc = tc.nc
    slots, nodes = tab.shape[1], x0.shape[1]
    half = BANK // 2

    pieces = [(0, 0, half), (0, half, half), (0, BANK, BANK), (1, 0, BANK), (1, BANK, half), (1, BANK + half, half)]
    count = len(pieces)
    in_block = [[i for i in range(count) if pieces[i][0] == block] for block in range(2)]
    on_vector = range(count - 3, count)

    with ExitStack() as ctx:
        held = ctx.enter_context(tc.tile_pool(name="held", bufs=1))
        diff_ring = ctx.enter_context(tc.tile_pool(name="diff_ring", bufs=3))
        psum = ctx.enter_context(tc.psum_pool(name="psum", bufs=8))

        def piece_tile(name, i):
            return held.tile([P, pieces[i][2]], F32, name=f"{name}_{i}")

        def psum_tile(i):
            return psum.tile([P, pieces[i][2]], F32, name="bank")

        def in_dram(array, i):
            block, first, width = pieces[i]
            return array[block * P : (block + 1) * P, first : first + width]

        offsets = held.tile(list(offs.shape), U16, name="offsets")
        nc.sync.dma_start(offsets[:], offs)
        identity = held.tile([P, P], F32, name="identity")
        make_identity(nc, identity[:])
        minus_identity = held.tile([P, P], F32, name="minus_identity")
        nc.gpsimd.tensor_scalar_mul(minus_identity[:], identity[:], -1.0)

        windows, own = {}, {}
        for block in range(2):
            windows[block] = held.tile([P, slots], F32, name=f"window{block}")
            nc.sync.dma_start(windows[block][:], tab[block * P : (block + 1) * P, :])
            for i in in_block[block]:
                own[i] = piece_tile("own", i)
                nc.sync.dma_start(own[i][:], in_dram(x0, i))

        def neighbour(i, d):
            block, first, width = pieces[i]
            column = (d * nodes + first) // GROUP
            return windows[block][:].indirect(offsets[:, column : column + width // GROUP])

        pair, mean, own_diff, variance, squares = {}, {}, {}, {}, {}

        for block in range(2):
            for i in in_block[block]:
                own_diff[i] = psum_tile(i)
                nc.tensor.matmul(own_diff[i][:], identity[:], own[i][:], start=True, stop=False)
            for i in in_block[block]:
                pair[i] = piece_tile("pair", i)
                nc.vector.tensor_tensor(pair[i][:], neighbour(i, 0), own[i][:], ADD)
            for i in in_block[block]:
                total = piece_tile("total", i)
                nc.vector.tensor_tensor(total[:], neighbour(i, 1), pair[i][:], ADD)
                mean[i] = piece_tile("mean", i)
                nc.scalar.activation(mean[i][:], total[:], COPY, scale=THIRD)
                nc.tensor.matmul(own_diff[i][:], minus_identity[:], mean[i][:], start=False, stop=True)

        def add_square(i, term, diff):
            square = squares[i, term] = piece_tile(f"square{term}", i)
            nc.scalar.activation(square[:], diff[:], SQUARE, scale=math.sqrt(THIRD))
            if i not in on_vector:
                if term == 0:
                    variance[i] = psum_tile(i)
                nc.tensor.matmul(variance[i][:], identity[:], square[:], start=term == 0, stop=term == 2)

        def neighbour_diff(i, d):
            diff = diff_ring.tile([P, pieces[i][2]], F32, name="diff")
            nc.vector.tensor_tensor(diff[:], neighbour(i, d), mean[i][:], SUBTRACT)
            return diff

        def finish(i):
            result = piece_tile("result", i)
            if i in on_vector:
                partial = piece_tile("partial", i)
                nc.vector.tensor_tensor(partial[:], squares[i, 0][:], squares[i, 1][:], ADD)
                nc.vector.tensor_tensor(result[:], partial[:], squares[i, 2][:], ADD)
                nc.sync.dma_start(in_dram(out, i), result[:])
            else:
                nc.scalar.activation(result[:], variance[i][:], COPY)
                nc.scalar.dma_start(in_dram(out, i), result[:])

        for i in range(count):
            add_square(i, 0, own_diff[i])
            add_square(i, 1, neighbour_diff(i, 0))
            if i > 0:
                finish(i - 1)
            add_square(i, 2, neighbour_diff(i, 1))
        finish(count - 1)
